import numpy as np
CORES = [3,0,2,1,6,7,4,5]
N = 8
ROOT = 6
def setup_inputs(rng):
    return {"x": rng.standard_normal((N, 128, 1024), dtype=np.float32)}
def reference(x):
    y = np.full((N, 128, N * 1024), np.nan, x.dtype)
    y[ROOT] = np.concatenate(list(x), axis=1)
    return {"y": y}

W = 1024
RANKS = 8
ENGINES = 16

SCRATCH = {
    "stage": ("sbuf", [128, W], "float32"),
    "land": ("sbuf", [128, RANKS * W], "float32"),
}
SEMAPHORES = ["loaded", "read", "arrived", "stored"]


def rank_program(g, core, T, topo):
    rank = T.rank_of(core)
    if rank is None:
        return
    root = T.root
    slot = slice(rank * W, (rank + 1) * W)

    if rank != root:
        root_core = T.cores[root]
        rid, pid, sengine = topo.addr(root_core)
        g.dma_start(T.stage[:], T.x[:]).then_inc(T.sem.loaded, 16)
        g.wait_ge(T.sem.loaded, 16)
        g.remote_dma(
            T.land[:, slot], T.stage[:],
            remote_sem=T.sem.arrived, local_sem=T.sem.read,
            pid=pid, routing_id=rid, dma_engine_mask=topo.mask(core, root_core),
        )
        g.wait_ge(T.sem.read, ENGINES)
        return

    g.dma_start(T.land[:, slot], T.x[:]).then_inc(T.sem.loaded, 16)
    g.wait_ge(T.sem.loaded, 16)
    g.wait_ge(T.sem.arrived, (RANKS - 1) * ENGINES)
    g.dma_start(T.y[:], T.land[:]).then_inc(T.sem.stored, 16)
    g.wait_ge(T.sem.stored, 16)
